import numpy as np
import ml_dtypes


def mxq(x, axis, fmt="e4m3"):
    dtype, down = {"e4m3": (ml_dtypes.float8_e4m3fn, 7), "e5m2": (ml_dtypes.float8_e5m2, 14)}[fmt]
    v = np.moveaxis(np.asarray(x, np.float32).astype(ml_dtypes.bfloat16).astype(np.float64), axis, -1)
    blocks = v.reshape(v.shape[:-1] + (-1, 32))
    amax = np.abs(blocks).max(-1, keepdims=True)
    byte = np.maximum(np.where(amax > 0, np.frexp(amax)[1] - 1 + 127, 0) - down, 1)
    scale = np.exp2(byte - 127.0)
    codes = (blocks / scale).astype(np.float32).astype(dtype).astype(np.float64)
    return np.moveaxis((codes * scale).reshape(v.shape), -1, axis)


WIDE = False


def mx_kscale(k):
    if not WIDE:
        return np.ones(k)
    levels = np.array([24, -24, 12, -12, 0])
    if k % 512:
        return np.exp2(np.random.permutation(np.resize(levels, k // 32))).repeat(32)
    a = np.empty((k // 512, 16))
    for p in range(k // 512):
        a[p, :8] = np.random.permutation(np.resize(levels, 8))
        for g in range(8):
            far = levels[np.abs(levels - a[p, g]) >= 10]
            a[p, g + 8] = far[np.random.randint(len(far))]
    return np.exp2(a.ravel()).repeat(32)


def f64(x):
    return np.asarray(x).astype(np.float64)


def striped8(idx):
    return np.concatenate([v.reshape(-1, 16).T for v in idx]).astype(np.uint16)


def unstriped8(offs):
    return np.stack([offs[16 * g:16 * g + 16].T.reshape(-1) for g in range(8)]).astype(np.int64)


K, N, T, J = 512, 512, 2048, 512


def setup_inputs():
    n = np.random.standard_normal
    s = mx_kscale(K)[:, None]
    return {
        "xT": (n((K, T)) * s).astype(np.float32),
        "wgt": np.repeat(np.random.uniform(0.5, 2.0, (8, 2 * J)), 16, axis=0).astype(np.float32),
        "w": (n((K, N)) / np.sqrt(K) / s).astype(np.float32),
        "b": (0.3 * n(N)).astype(np.float32),
        "offs": striped8(np.stack([np.concatenate([np.random.permutation(T)[:J] for _ in range(2)]) for _ in range(8)])),
    }


def reference(xT, wgt, w, b, offs):
    idx = unstriped8(offs)
    rows = np.arange(K)
    xg = f64(wgt)[rows // 4 % 128] * f64(xT)[rows[:, None], idx[rows % 512 // 64]]
    xT_ = mxq(xg, 0, "e4m3").reshape(K, 2, J)
    w_ = mxq(f64(w), 0, "e4m3")
    a0 = w_.T @ xT_[:, 0]
    a1 = w_.T @ xT_[:, 1]
    return a0 * a1 + f64(b)[:, None]

@@ -1,0 +1,184 @@
+from contextlib import ExitStack
+
+import concourse.mybir as mybir
+
+K, N, T, J = 512, 512, 2048, 512
+FLOPS = 2 * 2 * K * N * J
+
+F32 = mybir.dt.float32
+BF16 = mybir.dt.bfloat16
+U32 = mybir.dt.uint32
+U16 = mybir.dt.uint16
+U8 = mybir.dt.uint8
+FP8X4 = mybir.dt.float8_e4m3fn_x4
+MULT = mybir.AluOpType.mult
+ADD = mybir.AluOpType.add
+IDENTITY = mybir.ActivationFunctionType.Identity
+
+P = 128
+PACK = 4
+PICKS = 2
+HALF = J // 2
+GROUP = 16
+
+
+def tile_list_prod_bias_kernel(tc, xT, wgt, w, b, offs, out):
+    nc = tc.nc
+    with ExitStack() as ctx:
+        keep = ctx.enter_context(tc.tile_pool(name="keep", bufs=1))
+        psum = ctx.enter_context(tc.psum_pool(name="psum", bufs=1))
+
+        lists = keep.tile([P, PICKS * J // GROUP], U16, name="lists")
+        weights = [keep.tile([P, J], F32, name="weights%d" % c) for c in range(PICKS)]
+        rows = [keep.tile([P, T], F32, name="rows%d" % i) for i in range(PACK)]
+        picked = [keep.tile([P, PACK, J], F32, name="picked%d" % c) for c in range(PICKS)]
+        x_bf = [keep.tile([P, J, PACK], BF16, name="x_bf%d" % c, align_bytes=64) for c in range(PICKS)]
+        x_codes = [keep.tile([P, J], U32, name="x_codes%d" % c, align_bytes=64) for c in range(PICKS)]
+        x_scales = [keep.tile([P, J], U8, name="x_scales%d" % c, align_bytes=64) for c in range(PICKS)]
+        w_raw = [keep.tile([P, PACK, HALF], F32, name="w_raw%d" % u) for u in range(2)]
+        w_bf = [keep.tile([P, HALF, PACK], BF16, name="w_bf%d" % u, align_bytes=64) for u in range(2)]
+        w_codes = [keep.tile([P, HALF], U32, name="w_codes%d" % u, align_bytes=64) for u in range(2)]
+        w_scales = [keep.tile([P, HALF], U8, name="w_scales%d" % u, align_bytes=64) for u in range(2)]
+        bias = keep.tile([P, N // P], F32, name="bias")
+        sums = {}
+        first = {}
+        product = {}
+        result = {}
+        for h in range(2):
+            for u in range(2):
+                for c in range(PICKS):
+                    sums[c, h, u] = psum.tile([P, 2, HALF], F32, name="sums%d%d%d" % (c, h, u))
+                first[h, u] = keep.tile([P, 2, HALF], F32, name="first%d%d" % (h, u))
+                product[h, u] = keep.tile([P, 2, HALF], F32, name="product%d%d" % (h, u))
+                result[h, u] = keep.tile([P, 2, HALF], F32, name="result%d%d" % (h, u))
+
+        x_view = xT.rearrange("(p i) t -> p i t", i=PACK)
+        w_view = w.rearrange("(p i) n -> p i n", i=PACK)
+        out_view = out.rearrange("(m p) j -> p m j", p=P)
+
+        nc.sync.dma_start(lists[:], offs)
+        nc.sync.dma_start(weights[0][:], wgt[:, 0:J])
+        nc.sync.dma_start(rows[0][:], x_view[:, 0, :])
+        nc.sync.dma_start(weights[1][:], wgt[:, J : 2 * J])
+        for i in range(1, PACK):
+            nc.sync.dma_start(rows[i][:], x_view[:, i, :])
+        nc.sync.dma_start(w_raw[0][:], w_view[:, :, 0:HALF])
+        nc.sync.dma_start(w_raw[1][:], w_view[:, :, HALF:N])
+        with nc.allow_non_contiguous_dma(reason="one bias value to a partition"):
+            nc.sync.dma_start(bias[:], b.rearrange("(m p) -> p m", p=P))
+
+        def gather(i, c, lo, hi):
+            offsets = lists[:, (c * J + lo) // GROUP : (c * J + hi) // GROUP]
+            nc.vector.tensor_tensor(picked[c][:, i, lo:hi], rows[i][:].indirect(offsets), weights[c][:, lo:hi], MULT)
+
+        def round_pair(pair, c, lo, hi, copy):
+            copy(
+                x_bf[c][:, lo:hi, 2 * pair : 2 * pair + 2],
+                picked[c][:, 2 * pair : 2 * pair + 2, lo:hi].rearrange("p i j -> p j i"),
+            )
+
+        def round_w(u, copy):
+            copy(
+                w_bf[u][:].rearrange("p (a e) i -> p a i e", e=4),
+                w_raw[u][:].rearrange("p i (a e) -> p a i e", e=4),
+            )
+
+        def quantise_w(u):
+            nc.vector.quantize_mx(
+                out=w_codes[u][:].bitcast(FP8X4), scales=w_scales[u][:], in_=w_bf[u][:].rearrange("p n i -> p (n i)")
+            )
+
+        def quantise_x(c, h):
+            cols = slice(h * HALF, (h + 1) * HALF)
+            nc.vector.quantize_mx(
+                out=x_codes[c][:, cols].bitcast(FP8X4),
+                scales=x_scales[c][:, cols],
+                in_=x_bf[c][:, cols, :].rearrange("p j i -> p (j i)"),
+            )
+
+        def project(c, h, u):
+            cols = slice(h * HALF, (h + 1) * HALF)
+            for m in range(2):
+                chan = slice(m * P, (m + 1) * P)
+                nc.tensor.matmul_mx(
+                    out=sums[c, h, u][:, m, :],
+                    lhsT=w_codes[u][:, chan].bitcast(FP8X4),
+                    lhsT_scale=w_scales[u][:, chan],
+                    rhs=x_codes[c][:, cols].bitcast(FP8X4),
+                    rhs_scale=x_scales[c][:, cols],
+                    start=True,
+                    stop=True,
+                )
+
+        def keep_first(h, u):
+            nc.scalar.copy(first[h, u][:], sums[0, h, u][:])
+
+        def multiply(h, u, ms):
+            nc.vector.tensor_tensor(product[h, u][:, ms, :], sums[1, h, u][:, ms, :], first[h, u][:, ms, :], MULT)
+
+        def add_bias(h, u, m, on_vector):
+            column = bias[:, 2 * u + m : 2 * u + m + 1]
+            if on_vector:
+                nc.vector.tensor_scalar(result[h, u][:, m, :], product[h, u][:, m, :], column, None, ADD)
+            else:
+                nc.scalar.activation(result[h, u][:, m, :], product[h, u][:, m, :], IDENTITY, bias=column)
+
+        def store(h, u, ms):
+            nc.sync.dma_start(
+                out_view[:, 2 * u + ms.start : 2 * u + ms.stop, h * HALF : (h + 1) * HALF], result[h, u][:, ms, :]
+            )
+
+        on_v = nc.vector.tensor_copy
+        on_s = nc.scalar.copy
+        both = slice(0, 2)
+        for i in range(2):
+            for c in range(PICKS):
+                gather(i, c, 0, J)
+        for c in range(PICKS):
+            round_pair(0, c, 0, J, on_s)
+        for c in range(PICKS):
+            gather(2, c, 0, J)
+        gather(3, 0, 0, HALF)
+        round_w(0, on_s)
+        gather(3, 1, 0, HALF)
+        round_pair(1, 0, 0, HALF, on_v)
+        round_pair(1, 1, 0, HALF, on_s)
+        gather(3, 0, HALF, J)
+        quantise_w(0)
+        round_w(1, on_s)
+        quantise_x(0, 0)
+        quantise_x(1, 0)
+        project(0, 0, 0)
+        project(1, 0, 0)
+        gather(3, 1, HALF, J)
+        round_pair(1, 0, HALF, J, on_s)
+        quantise_w(1)
+        round_pair(1, 1, HALF, J, on_v)
+        keep_first(0, 0)
+        project(0, 0, 1)
+        quantise_x(0, 1)
+        project(1, 0, 1)
+        quantise_x(1, 1)
+        keep_first(0, 1)
+        multiply(0, 0, both)
+        project(0, 1, 0)
+        project(0, 1, 1)
+        multiply(0, 1, both)
+        keep_first(1, 0)
+        project(1, 1, 0)
+        project(1, 1, 1)
+        keep_first(1, 1)
+        add_bias(0, 0, 0, True)
+        add_bias(0, 0, 1, True)
+        store(0, 0, both)
+        add_bias(0, 1, 0, True)
+        add_bias(0, 1, 1, False)
+        store(0, 1, both)
+        multiply(1, 0, both)
+        add_bias(1, 0, 0, False)
+        add_bias(1, 0, 1, False)
+        store(1, 0, both)
+        for m in range(2):
+            multiply(1, 1, slice(m, m + 1))
+            add_bias(1, 1, m, False)
+            store(1, 1, slice(m, m + 1))

@@ -56,9 +56,9 @@ def tile_list_prod_bias_kernel(tc, xT, wgt, w, b, offs, out):
         w_view = w.rearrange("(p i) n -> p i n", i=PACK)
         out_view = out.rearrange("(m p) j -> p m j", p=P)
 
+        nc.sync.dma_start(rows[0][:], x_view[:, 0, :])
         nc.sync.dma_start(lists[:], offs)
         nc.sync.dma_start(weights[0][:], wgt[:, 0:J])
-        nc.sync.dma_start(rows[0][:], x_view[:, 0, :])
         nc.sync.dma_start(weights[1][:], wgt[:, J : 2 * J])
         for i in range(1, PACK):
             nc.sync.dma_start(rows[i][:], x_view[:, i, :])
@@ -110,8 +110,8 @@ def tile_list_prod_bias_kernel(tc, xT, wgt, w, b, offs, out):
                     stop=True,
                 )
 
-        def keep_first(h, u):
-            nc.scalar.copy(first[h, u][:], sums[0, h, u][:])
+        def keep_first(h, u, copy):
+            copy(first[h, u][:], sums[0, h, u][:])
 
         def multiply(h, u, ms):
             nc.vector.tensor_tensor(product[h, u][:, ms, :], sums[1, h, u][:, ms, :], first[h, u][:, ms, :], MULT)
@@ -138,46 +138,40 @@ def tile_list_prod_bias_kernel(tc, xT, wgt, w, b, offs, out):
             round_pair(0, c, 0, J, on_s)
         for c in range(PICKS):
             gather(2, c, 0, J)
-        gather(3, 0, 0, HALF)
-        round_w(0, on_s)
-        gather(3, 1, 0, HALF)
-        round_pair(1, 0, 0, HALF, on_v)
-        round_pair(1, 1, 0, HALF, on_s)
-        gather(3, 0, HALF, J)
-        quantise_w(0)
-        round_w(1, on_s)
+        for h in range(2):
+            for c in range(PICKS):
+                gather(3, c, h * HALF, (h + 1) * HALF)
+                round_pair(1, c, h * HALF, (h + 1) * HALF, on_s)
+        round_w(0, on_v)
         quantise_x(0, 0)
+        quantise_w(0)
         quantise_x(1, 0)
-        project(0, 0, 0)
-        project(1, 0, 0)
-        gather(3, 1, HALF, J)
-        round_pair(1, 0, HALF, J, on_s)
-        quantise_w(1)
-        round_pair(1, 1, HALF, J, on_v)
-        keep_first(0, 0)
-        project(0, 0, 1)
         quantise_x(0, 1)
-        project(1, 0, 1)
         quantise_x(1, 1)
-        keep_first(0, 1)
+        round_w(1, on_s)
+        for h in range(2):
+            for c in range(PICKS):
+                project(c, h, 0)
+        keep_first(0, 0, on_v)
+        quantise_w(1)
+        for c in range(PICKS):
+            for h in range(2):
+                project(c, h, 1)
+        keep_first(1, 0, on_s)
         multiply(0, 0, both)
-        project(0, 1, 0)
-        project(0, 1, 1)
-        multiply(0, 1, both)
-        keep_first(1, 0)
-        project(1, 1, 0)
-        project(1, 1, 1)
-        keep_first(1, 1)
+        multiply(1, 0, both)
+        keep_first(0, 1, on_s)
+        keep_first(1, 1, on_s)
         add_bias(0, 0, 0, True)
-        add_bias(0, 0, 1, True)
+        add_bias(0, 0, 1, False)
         store(0, 0, both)
+        add_bias(1, 0, 0, True)
+        add_bias(1, 0, 1, True)
+        store(1, 0, both)
+        multiply(0, 1, both)
         add_bias(0, 1, 0, True)
         add_bias(0, 1, 1, False)
         store(0, 1, both)
-        multiply(1, 0, both)
-        add_bias(1, 0, 0, False)
-        add_bias(1, 0, 1, False)
-        store(1, 0, both)
         for m in range(2):
             multiply(1, 1, slice(m, m + 1))
             add_bias(1, 1, m, False)

@@ -158,21 +158,12 @@ def tile_list_prod_bias_kernel(tc, xT, wgt, w, b, offs, out):
             for h in range(2):
                 project(c, h, 1)
         keep_first(1, 0, on_s)
-        multiply(0, 0, both)
-        multiply(1, 0, both)
-        keep_first(0, 1, on_s)
-        keep_first(1, 1, on_s)
-        add_bias(0, 0, 0, True)
-        add_bias(0, 0, 1, False)
-        store(0, 0, both)
-        add_bias(1, 0, 0, True)
-        add_bias(1, 0, 1, True)
-        store(1, 0, both)
-        multiply(0, 1, both)
-        add_bias(0, 1, 0, True)
-        add_bias(0, 1, 1, False)
-        store(0, 1, both)
-        for m in range(2):
-            multiply(1, 1, slice(m, m + 1))
-            add_bias(1, 1, m, False)
-            store(1, 1, slice(m, m + 1))
+        for u in range(2):
+            for h in range(2):
+                if u == 1:
+                    keep_first(h, u, on_s)
+            for h in range(2):
+                for m in range(2):
+                    multiply(h, u, slice(m, m + 1))
+                    add_bias(h, u, m, (h, u) == (1, 0))
+                    store(h, u, slice(m, m + 1))

@@ -20,6 +20,8 @@ PACK = 4
 PICKS = 2
 HALF = J // 2
 GROUP = 16
+BLOCK = 32
+QUARTER = J // 4
 
 
 def tile_list_prod_bias_kernel(tc, xT, wgt, w, b, offs, out):
@@ -29,13 +31,17 @@ def tile_list_prod_bias_kernel(tc, xT, wgt, w, b, offs, out):
         psum = ctx.enter_context(tc.psum_pool(name="psum", bufs=1))
 
         lists = keep.tile([P, PICKS * J // GROUP], U16, name="lists")
-        weights = [keep.tile([P, J], F32, name="weights%d" % c) for c in range(PICKS)]
+        weights = [keep.tile([P, J], F32, name="weights%d" % c, align_bytes=64) for c in range(PICKS)]
+        wgt_rows = keep.tile([P, 2, BLOCK], F32, name="wgt_rows", align_bytes=64)
+        wgt_turned = keep.tile([P, 2, 2, GROUP], F32, name="wgt_turned", align_bytes=64)
+        wgt_wide = [keep.tile([P, 8, 2, 2, GROUP], F32, name="wgt_wide%d" % c, align_bytes=64) for c in range(PICKS)]
         rows = [keep.tile([P, T], F32, name="rows%d" % i) for i in range(PACK)]
-        picked = [keep.tile([P, PACK, J], F32, name="picked%d" % c) for c in range(PICKS)]
-        x_bf = [keep.tile([P, J, PACK], BF16, name="x_bf%d" % c, align_bytes=64) for c in range(PICKS)]
+        early = [keep.tile([P, 2, J], F32, name="early%d" % c) for c in range(PICKS)]
+        late = keep.tile([P, 14, QUARTER], F32, name="late")
+        x_bf = {}
         x_codes = [keep.tile([P, J], U32, name="x_codes%d" % c, align_bytes=64) for c in range(PICKS)]
         x_scales = [keep.tile([P, J], U8, name="x_scales%d" % c, align_bytes=64) for c in range(PICKS)]
-        w_raw = [keep.tile([P, PACK, HALF], F32, name="w_raw%d" % u) for u in range(2)]
+        w_raw = [keep.tile([P, PACK, HALF], F32, name="w_raw%d" % u, tag="w_raw%d" % u, align_bytes=64) for u in range(2)]
         w_bf = [keep.tile([P, HALF, PACK], BF16, name="w_bf%d" % u, align_bytes=64) for u in range(2)]
         w_codes = [keep.tile([P, HALF], U32, name="w_codes%d" % u, align_bytes=64) for u in range(2)]
         w_scales = [keep.tile([P, HALF], U8, name="w_scales%d" % u, align_bytes=64) for u in range(2)]
@@ -56,26 +62,42 @@ def tile_list_prod_bias_kernel(tc, xT, wgt, w, b, offs, out):
         w_view = w.rearrange("(p i) n -> p i n", i=PACK)
         out_view = out.rearrange("(m p) j -> p m j", p=P)
 
-        nc.sync.dma_start(rows[0][:], x_view[:, 0, :])
+        nc.sync.dma_start(
+            wgt_rows[:].rearrange("p b e -> p (b e)"),
+            wgt.rearrange("(g s) (r e) -> g s r e", s=GROUP, r=GROUP)[:, 0, :, :],
+        )
         nc.sync.dma_start(lists[:], offs)
-        nc.sync.dma_start(weights[0][:], wgt[:, 0:J])
-        nc.sync.dma_start(weights[1][:], wgt[:, J : 2 * J])
-        for i in range(1, PACK):
-            nc.sync.dma_start(rows[i][:], x_view[:, i, :])
+        nc.sync.dma_start(rows[0][:], x_view[:, 0, :])
+        nc.sync.dma_start(rows[1][:], x_view[:, 1, :])
         nc.sync.dma_start(w_raw[0][:], w_view[:, :, 0:HALF])
+        nc.sync.dma_start(rows[2][:], x_view[:, 2, :])
         nc.sync.dma_start(w_raw[1][:], w_view[:, :, HALF:N])
+        nc.sync.dma_start(rows[3][:], x_view[:, 3, :])
         with nc.allow_non_contiguous_dma(reason="one bias value to a partition"):
             nc.sync.dma_start(bias[:], b.rearrange("(m p) -> p m", p=P))
 
-        def gather(i, c, lo, hi):
-            offsets = lists[:, (c * J + lo) // GROUP : (c * J + hi) // GROUP]
-            nc.vector.tensor_tensor(picked[c][:, i, lo:hi], rows[i][:].indirect(offsets), weights[c][:, lo:hi], MULT)
+        def spread_weights(c, copy):
+            source = wgt_turned[:].rearrange("p b h r -> p r b h")[:, 8 * c : 8 * c + 8, :, :]
+            copy(wgt_wide[c][:], source.unsqueeze(4).to_broadcast([P, 8, 2, 2, GROUP]))
+            nc.vector.transpose(weights[c][:], wgt_wide[c][:].rearrange("p r b h s -> p (r b h s)"))
 
-        def round_pair(pair, c, lo, hi, copy):
-            copy(
-                x_bf[c][:, lo:hi, 2 * pair : 2 * pair + 2],
-                picked[c][:, 2 * pair : 2 * pair + 2, lo:hi].rearrange("p i j -> p j i"),
-            )
+        def gather(i, c, lo, hi, target):
+            offsets = lists[:, (c * J + lo) // GROUP : (c * J + hi) // GROUP]
+            nc.vector.tensor_tensor(target, rows[i][:].indirect(offsets), weights[c][:, lo:hi], MULT)
+
+        def late_view(width):
+            return late[:].rearrange("p (s t) j -> p s (t j)", t=width // QUARTER)
+
+        def gather_last(c, lo, width, slot):
+            gather(3, c, lo, lo + width, late_view(width)[:, slot, :])
+
+        def round_early(c, copy):
+            copy(x_bf[c][:, :, 0:2], early[c][:].rearrange("p i j -> p j i"))
+
+        def round_late(c, lo, width, slot, copy):
+            a = (c * J + lo) // width
+            pair = late_view(width)[:, a : slot + 1 : slot - a, :]
+            copy(x_bf[c][:, lo : lo + width, 2:4], pair.rearrange("p i j -> p j i"))
 
         def round_w(u, copy):
             copy(
@@ -88,38 +110,47 @@ def tile_list_prod_bias_kernel(tc, xT, wgt, w, b, offs, out):
                 out=w_codes[u][:].bitcast(FP8X4), scales=w_scales[u][:], in_=w_bf[u][:].rearrange("p n i -> p (n i)")
             )
 
-        def quantise_x(c, h):
-            cols = slice(h * HALF, (h + 1) * HALF)
+        def quantise_x(c, lo, width):
+            cols = slice(lo, lo + width)
             nc.vector.quantize_mx(
                 out=x_codes[c][:, cols].bitcast(FP8X4),
                 scales=x_scales[c][:, cols],
                 in_=x_bf[c][:, cols, :].rearrange("p j i -> p (j i)"),
             )
 
-        def project(c, h, u):
-            cols = slice(h * HALF, (h + 1) * HALF)
-            for m in range(2):
-                chan = slice(m * P, (m + 1) * P)
-                nc.tensor.matmul_mx(
-                    out=sums[c, h, u][:, m, :],
-                    lhsT=w_codes[u][:, chan].bitcast(FP8X4),
-                    lhsT_scale=w_scales[u][:, chan],
-                    rhs=x_codes[c][:, cols].bitcast(FP8X4),
-                    rhs_scale=x_scales[c][:, cols],
-                    start=True,
-                    stop=True,
-                )
+        def bank(c, h, u, m):
+            if (c, h, u, m) == (1, 1, 1, 1):
+                return sums[0, 0, 0][:, 0, :]
+            return sums[c, h, u][:, m, :]
+
+        def project(c, lo, width):
+            cols = slice(lo, lo + width)
+            h = lo // HALF
+            for u in range(2):
+                for m in range(2):
+                    chan = slice(m * P, (m + 1) * P)
+                    nc.tensor.matmul_mx(
+                        out=bank(c, h, u, m)[:, lo - h * HALF : lo - h * HALF + width],
+                        lhsT=w_codes[u][:, chan].bitcast(FP8X4),
+                        lhsT_scale=w_scales[u][:, chan],
+                        rhs=x_codes[c][:, cols].bitcast(FP8X4),
+                        rhs_scale=x_scales[c][:, cols],
+                        start=True,
+                        stop=True,
+                    )
 
         def keep_first(h, u, copy):
             copy(first[h, u][:], sums[0, h, u][:])
 
-        def multiply(h, u, ms):
-            nc.vector.tensor_tensor(product[h, u][:, ms, :], sums[1, h, u][:, ms, :], first[h, u][:, ms, :], MULT)
+        def multiply(h, u, m):
+            nc.vector.tensor_tensor(product[h, u][:, m, :], bank(1, h, u, m), first[h, u][:, m, :], MULT)
 
-        def add_bias(h, u, m, on_vector):
+        def add_bias(h, u, m, engine):
             column = bias[:, 2 * u + m : 2 * u + m + 1]
-            if on_vector:
+            if engine == "v":
                 nc.vector.tensor_scalar(result[h, u][:, m, :], product[h, u][:, m, :], column, None, ADD)
+            elif engine == "g":
+                nc.gpsimd.tensor_scalar(result[h, u][:, m, :], product[h, u][:, m, :], 1.0, column, MULT, ADD)
             else:
                 nc.scalar.activation(result[h, u][:, m, :], product[h, u][:, m, :], IDENTITY, bias=column)
 
@@ -130,40 +161,47 @@ def tile_list_prod_bias_kernel(tc, xT, wgt, w, b, offs, out):
 
         on_v = nc.vector.tensor_copy
         on_s = nc.scalar.copy
-        both = slice(0, 2)
+        for half in range(2):
+            nc.vector.transpose(wgt_turned[:, half, :, :].rearrange("p h r -> p (h r)"), wgt_rows[:, half, :])
+        spread_weights(0, on_v)
+        spread_weights(1, on_s)
         for i in range(2):
             for c in range(PICKS):
-                gather(i, c, 0, J)
+                gather(i, c, 0, J, early[c][:, i, :])
         for c in range(PICKS):
-            round_pair(0, c, 0, J, on_s)
+            round_w(c, on_s)
+            quantise_w(c)
+            x_bf[c] = keep.tile([P, J, PACK], BF16, name="x_bf%d" % c, tag="w_raw%d" % c, align_bytes=64)
+            round_early(c, on_s)
         for c in range(PICKS):
-            gather(2, c, 0, J)
-        for h in range(2):
-            for c in range(PICKS):
-                gather(3, c, h * HALF, (h + 1) * HALF)
-                round_pair(1, c, h * HALF, (h + 1) * HALF, on_s)
-        round_w(0, on_v)
-        quantise_x(0, 0)
-        quantise_w(0)
-        quantise_x(1, 0)
-        quantise_x(0, 1)
-        quantise_x(1, 1)
-        round_w(1, on_s)
-        for h in range(2):
-            for c in range(PICKS):
-                project(c, h, 0)
-        keep_first(0, 0, on_v)
-        quantise_w(1)
-        for c in range(PICKS):
-            for h in range(2):
-                project(c, h, 1)
-        keep_first(1, 0, on_s)
+            gather(2, c, 0, J, late[:, 4 * c : 4 * c + 4, :].rearrange("p s j -> p (s j)"))
+        def finish(h, u, engines):
+            for m in range(2):
+                multiply(h, u, m)
+                add_bias(h, u, m, engines[m])
+                store(h, u, slice(m, m + 1))
+
+        def pick(c, lo, width, slot, copy):
+            gather_last(c, lo, width, slot)
+            round_late(c, lo, width, slot, copy)
+
+        def contract(c, lo, width):
+            quantise_x(c, lo, width)
+            project(c, lo, width)
+
+        pick(0, 0, HALF, 4, on_s)
+        pick(1, 0, HALF, 5, on_s)
+        pick(0, HALF, HALF, 6, on_s)
+        contract(0, 0, HALF)
+        pick(1, HALF, HALF, 4, on_v)
+        contract(1, 0, HALF)
         for u in range(2):
-            for h in range(2):
-                if u == 1:
-                    keep_first(h, u, on_s)
-            for h in range(2):
-                for m in range(2):
-                    multiply(h, u, slice(m, m + 1))
-                    add_bias(h, u, m, (h, u) == (1, 0))
-                    store(h, u, slice(m, m + 1))
+            keep_first(0, u, on_s)
+        contract(0, HALF, HALF)
+        for u in range(2):
+            keep_first(1, u, on_s)
+        contract(1, HALF, HALF)
+        finish(0, 0, "gg")
+        finish(0, 1, "vg")
+        finish(1, 0, "ss")
+        finish(1, 1, "sv")

@@ -21,7 +21,6 @@ PICKS = 2
 HALF = J // 2
 GROUP = 16
 BLOCK = 32
-QUARTER = J // 4
 
 
 def tile_list_prod_bias_kernel(tc, xT, wgt, w, b, offs, out):
@@ -37,11 +36,12 @@ def tile_list_prod_bias_kernel(tc, xT, wgt, w, b, offs, out):
         wgt_wide = [keep.tile([P, 8, 2, 2, GROUP], F32, name="wgt_wide%d" % c, align_bytes=64) for c in range(PICKS)]
         rows = [keep.tile([P, T], F32, name="rows%d" % i) for i in range(PACK)]
         early = [keep.tile([P, 2, J], F32, name="early%d" % c) for c in range(PICKS)]
-        late = keep.tile([P, 14, QUARTER], F32, name="late")
-        x_bf = {}
+        late = keep.tile([P, 10, HALF], F32, name="late")
+        x_bf = [keep.tile([P, J, PACK], BF16, name="x_bf%d" % c, align_bytes=64) for c in range(PICKS)]
         x_codes = [keep.tile([P, J], U32, name="x_codes%d" % c, align_bytes=64) for c in range(PICKS)]
         x_scales = [keep.tile([P, J], U8, name="x_scales%d" % c, align_bytes=64) for c in range(PICKS)]
-        w_raw = [keep.tile([P, PACK, HALF], F32, name="w_raw%d" % u, tag="w_raw%d" % u, align_bytes=64) for u in range(2)]
+        w_second = keep.tile([P, PACK, HALF], F32, name="w_second")
+        w_raw = [late[:, 3:7, :], w_second[:]]
         w_bf = [keep.tile([P, HALF, PACK], BF16, name="w_bf%d" % u, align_bytes=64) for u in range(2)]
         w_codes = [keep.tile([P, HALF], U32, name="w_codes%d" % u, align_bytes=64) for u in range(2)]
         w_scales = [keep.tile([P, HALF], U8, name="w_scales%d" % u, align_bytes=64) for u in range(2)]
@@ -66,13 +66,13 @@ def tile_list_prod_bias_kernel(tc, xT, wgt, w, b, offs, out):
             wgt_rows[:].rearrange("p b e -> p (b e)"),
             wgt.rearrange("(g s) (r e) -> g s r e", s=GROUP, r=GROUP)[:, 0, :, :],
         )
-        nc.sync.dma_start(lists[:], offs)
         nc.sync.dma_start(rows[0][:], x_view[:, 0, :])
+        nc.sync.dma_start(lists[:], offs)
         nc.sync.dma_start(rows[1][:], x_view[:, 1, :])
-        nc.sync.dma_start(w_raw[0][:], w_view[:, :, 0:HALF])
         nc.sync.dma_start(rows[2][:], x_view[:, 2, :])
-        nc.sync.dma_start(w_raw[1][:], w_view[:, :, HALF:N])
         nc.sync.dma_start(rows[3][:], x_view[:, 3, :])
+        nc.sync.dma_start(w_raw[0], w_view[:, :, 0:HALF])
+        nc.sync.dma_start(w_raw[1], w_view[:, :, HALF:N])
         with nc.allow_non_contiguous_dma(reason="one bias value to a partition"):
             nc.sync.dma_start(bias[:], b.rearrange("(m p) -> p m", p=P))
 
@@ -85,24 +85,21 @@ def tile_list_prod_bias_kernel(tc, xT, wgt, w, b, offs, out):
             offsets = lists[:, (c * J + lo) // GROUP : (c * J + hi) // GROUP]
             nc.vector.tensor_tensor(target, rows[i][:].indirect(offsets), weights[c][:, lo:hi], MULT)
 
-        def late_view(width):
-            return late[:].rearrange("p (s t) j -> p s (t j)", t=width // QUARTER)
-
-        def gather_last(c, lo, width, slot):
-            gather(3, c, lo, lo + width, late_view(width)[:, slot, :])
+        def gather_half(i, c, h, slot):
+            gather(i, c, h * HALF, (h + 1) * HALF, late[:, slot, :])
 
         def round_early(c, copy):
             copy(x_bf[c][:, :, 0:2], early[c][:].rearrange("p i j -> p j i"))
 
-        def round_late(c, lo, width, slot, copy):
-            a = (c * J + lo) // width
-            pair = late_view(width)[:, a : slot + 1 : slot - a, :]
-            copy(x_bf[c][:, lo : lo + width, 2:4], pair.rearrange("p i j -> p j i"))
+        def round_late(c, h, slot, copy):
+            a = PICKS * c + h
+            pair = late[:, a : slot + 1 : slot - a, :]
+            copy(x_bf[c][:, h * HALF : (h + 1) * HALF, 2:4], pair.rearrange("p i j -> p j i"))
 
         def round_w(u, copy):
             copy(
                 w_bf[u][:].rearrange("p (a e) i -> p a i e", e=4),
-                w_raw[u][:].rearrange("p i (a e) -> p a i e", e=4),
+                w_raw[u].rearrange("p i (a e) -> p a i e", e=4),
             )
 
         def quantise_w(u):
@@ -110,8 +107,8 @@ def tile_list_prod_bias_kernel(tc, xT, wgt, w, b, offs, out):
                 out=w_codes[u][:].bitcast(FP8X4), scales=w_scales[u][:], in_=w_bf[u][:].rearrange("p n i -> p (n i)")
             )
 
-        def quantise_x(c, lo, width):
-            cols = slice(lo, lo + width)
+        def quantise_x(c, h):
+            cols = slice(h * HALF, (h + 1) * HALF)
             nc.vector.quantize_mx(
                 out=x_codes[c][:, cols].bitcast(FP8X4),
                 scales=x_scales[c][:, cols],
@@ -123,21 +120,19 @@ def tile_list_prod_bias_kernel(tc, xT, wgt, w, b, offs, out):
                 return sums[0, 0, 0][:, 0, :]
             return sums[c, h, u][:, m, :]
 
-        def project(c, lo, width):
-            cols = slice(lo, lo + width)
-            h = lo // HALF
-            for u in range(2):
-                for m in range(2):
-                    chan = slice(m * P, (m + 1) * P)
-                    nc.tensor.matmul_mx(
-                        out=bank(c, h, u, m)[:, lo - h * HALF : lo - h * HALF + width],
-                        lhsT=w_codes[u][:, chan].bitcast(FP8X4),
-                        lhsT_scale=w_scales[u][:, chan],
-                        rhs=x_codes[c][:, cols].bitcast(FP8X4),
-                        rhs_scale=x_scales[c][:, cols],
-                        start=True,
-                        stop=True,
-                    )
+        def project(c, h, u):
+            cols = slice(h * HALF, (h + 1) * HALF)
+            for m in range(2):
+                chan = slice(m * P, (m + 1) * P)
+                nc.tensor.matmul_mx(
+                    out=bank(c, h, u, m),
+                    lhsT=w_codes[u][:, chan].bitcast(FP8X4),
+                    lhsT_scale=w_scales[u][:, chan],
+                    rhs=x_codes[c][:, cols].bitcast(FP8X4),
+                    rhs_scale=x_scales[c][:, cols],
+                    start=True,
+                    stop=True,
+                )
 
         def keep_first(h, u, copy):
             copy(first[h, u][:], sums[0, h, u][:])
@@ -161,6 +156,12 @@ def tile_list_prod_bias_kernel(tc, xT, wgt, w, b, offs, out):
 
         on_v = nc.vector.tensor_copy
         on_s = nc.scalar.copy
+        def finish(h, u, engines):
+            for m in range(2):
+                multiply(h, u, m)
+                add_bias(h, u, m, engines[m])
+                store(h, u, slice(m, m + 1))
+
         for half in range(2):
             nc.vector.transpose(wgt_turned[:, half, :, :].rearrange("p h r -> p (h r)"), wgt_rows[:, half, :])
         spread_weights(0, on_v)
@@ -169,39 +170,39 @@ def tile_list_prod_bias_kernel(tc, xT, wgt, w, b, offs, out):
             for c in range(PICKS):
                 gather(i, c, 0, J, early[c][:, i, :])
         for c in range(PICKS):
-            round_w(c, on_s)
-            quantise_w(c)
-            x_bf[c] = keep.tile([P, J, PACK], BF16, name="x_bf%d" % c, tag="w_raw%d" % c, align_bytes=64)
             round_early(c, on_s)
-        for c in range(PICKS):
-            gather(2, c, 0, J, late[:, 4 * c : 4 * c + 4, :].rearrange("p s j -> p (s j)"))
-        def finish(h, u, engines):
-            for m in range(2):
-                multiply(h, u, m)
-                add_bias(h, u, m, engines[m])
-                store(h, u, slice(m, m + 1))
-
-        def pick(c, lo, width, slot, copy):
-            gather_last(c, lo, width, slot)
-            round_late(c, lo, width, slot, copy)
-
-        def contract(c, lo, width):
-            quantise_x(c, lo, width)
-            project(c, lo, width)
-
-        pick(0, 0, HALF, 4, on_s)
-        pick(1, 0, HALF, 5, on_s)
-        pick(0, HALF, HALF, 6, on_s)
-        contract(0, 0, HALF)
-        pick(1, HALF, HALF, 4, on_v)
-        contract(1, 0, HALF)
-        for u in range(2):
-            keep_first(0, u, on_s)
-        contract(0, HALF, HALF)
-        for u in range(2):
-            keep_first(1, u, on_s)
-        contract(1, HALF, HALF)
-        finish(0, 0, "gg")
-        finish(0, 1, "vg")
+        gather(2, 0, 0, J, late[:, 0:2, :].rearrange("p s j -> p (s j)"))
+        gather_half(2, 1, 0, 2)
+        gather_half(3, 0, 0, 7)
+        round_late(0, 0, 7, on_s)
+        gather_half(3, 1, 0, 8)
+        round_late(1, 0, 8, on_s)
+        gather_half(3, 0, 1, 9)
+        round_late(0, 1, 9, on_s)
+        round_w(0, on_v)
+        quantise_x(0, 0)
+        quantise_w(0)
+        quantise_x(1, 0)
+        project(0, 0, 0)
+        project(1, 0, 0)
+        round_w(1, on_s)
+        keep_first(0, 0, on_s)
+        gather_half(2, 1, 1, 3)
+        gather_half(3, 1, 1, 8)
+        quantise_x(0, 1)
+        project(0, 1, 0)
+        round_late(1, 1, 8, on_v)
+        quantise_w(1)
+        project(0, 0, 1)
+        project(1, 0, 1)
+        project(0, 1, 1)
+        quantise_x(1, 1)
+        project(1, 1, 0)
+        project(1, 1, 1)
+        keep_first(1, 0, on_s)
+        keep_first(0, 1, on_s)
+        keep_first(1, 1, on_s)
+        finish(0, 0, "vv")
         finish(1, 0, "ss")
+        finish(0, 1, "ss")
         finish(1, 1, "sv")

@@ -31,9 +31,15 @@ def tile_list_prod_bias_kernel(tc, xT, wgt, w, b, offs, out):
 
         lists = keep.tile([P, PICKS * J // GROUP], U16, name="lists")
         weights = [keep.tile([P, J], F32, name="weights%d" % c, align_bytes=64) for c in range(PICKS)]
-        wgt_rows = keep.tile([P, 2, BLOCK], F32, name="wgt_rows", align_bytes=64)
-        wgt_turned = keep.tile([P, 2, 2, GROUP], F32, name="wgt_turned", align_bytes=64)
-        wgt_wide = [keep.tile([P, 8, 2, 2, GROUP], F32, name="wgt_wide%d" % c, align_bytes=64) for c in range(PICKS)]
+        wgt_rows = keep.tile([P, BLOCK], F32, name="wgt_rows", align_bytes=64)
+        wgt_turned = keep.tile([P, 2, GROUP], F32, name="wgt_turned", align_bytes=64)
+        wgt_wide = keep.tile([P, GROUP, 2, GROUP], F32, name="wgt_wide", align_bytes=64)
+        wgt_rows1 = keep.tile([P, P], F32, name="wgt_rows1")
+        wgt_wide1 = keep.tile([P, 4, 8, GROUP], F32, name="wgt_wide1")
+        identity = keep.tile([P, P], F32, name="identity")
+        ones = keep.tile([P, BLOCK], F32, name="ones")
+        ramp = keep.tile([P, BLOCK], F32, name="ramp", align_bytes=64)
+        ramp_turned = keep.tile([P, BLOCK], F32, name="ramp_turned", align_bytes=64)
         rows = [keep.tile([P, T], F32, name="rows%d" % i) for i in range(PACK)]
         early = [keep.tile([P, 2, J], F32, name="early%d" % c) for c in range(PICKS)]
         late = keep.tile([P, 10, HALF], F32, name="late")
@@ -62,10 +68,9 @@ def tile_list_prod_bias_kernel(tc, xT, wgt, w, b, offs, out):
         w_view = w.rearrange("(p i) n -> p i n", i=PACK)
         out_view = out.rearrange("(m p) j -> p m j", p=P)
 
-        nc.sync.dma_start(
-            wgt_rows[:].rearrange("p b e -> p (b e)"),
-            wgt.rearrange("(g s) (r e) -> g s r e", s=GROUP, r=GROUP)[:, 0, :, :],
-        )
+        head_rows = wgt.rearrange("(g s) j -> g s j", s=GROUP)[:, 0, :]
+        nc.sync.dma_start(wgt_rows[:], head_rows[:, 0:J].rearrange("g (r e) -> g r e", e=BLOCK))
+        nc.sync.dma_start(wgt_rows1[0:32, :], head_rows[:, J : 2 * J].rearrange("g (a e) -> g a e", e=P))
         nc.sync.dma_start(rows[0][:], x_view[:, 0, :])
         nc.sync.dma_start(lists[:], offs)
         nc.sync.dma_start(rows[1][:], x_view[:, 1, :])
@@ -76,10 +81,34 @@ def tile_list_prod_bias_kernel(tc, xT, wgt, w, b, offs, out):
         with nc.allow_non_contiguous_dma(reason="one bias value to a partition"):
             nc.sync.dma_start(bias[:], b.rearrange("(m p) -> p m", p=P))
 
-        def spread_weights(c, copy):
-            source = wgt_turned[:].rearrange("p b h r -> p r b h")[:, 8 * c : 8 * c + 8, :, :]
-            copy(wgt_wide[c][:], source.unsqueeze(4).to_broadcast([P, 8, 2, 2, GROUP]))
-            nc.vector.transpose(weights[c][:], wgt_wide[c][:].rearrange("p r b h s -> p (r b h s)"))
+        def spread_first():
+            nc.vector.transpose(wgt_turned[:].rearrange("p h r -> p (h r)"), wgt_rows[:])
+            source = wgt_turned[:].rearrange("p h r -> p r h").unsqueeze(3)
+            nc.vector.tensor_copy(wgt_wide[:], source.to_broadcast([P, GROUP, 2, GROUP]))
+            nc.vector.transpose(weights[0][:], wgt_wide[:].rearrange("p r h s -> p (r h s)"))
+
+        def spread_second():
+            nc.vector.memset(ones[:], 1.0)
+            nc.vector.memset(identity[:], 0.0)
+            nc.vector.tensor_tensor_scan(ramp[:], ones[:], ones[:], 0.0, MULT, ADD)
+            nc.vector.transpose(ramp_turned[:], ramp[:])
+            for q in range(P // BLOCK):
+                part = slice(q * BLOCK, (q + 1) * BLOCK)
+                nc.vector.tensor_tensor(
+                    identity[part, part], ramp[part, :], ramp_turned[part, :], mybir.AluOpType.is_equal
+                )
+            nc.vector.memset(wgt_rows1[32:64, :], 0.0)
+            nc.vector.memset(wgt_rows1[64:128, :], 0.0)
+            turned = sums[1, 1, 0][:, 0, 0:P]
+            nc.tensor.transpose(turned, wgt_rows1[:], identity[:])
+            source = turned[:, 0:32].rearrange("p (g a) -> p a g", a=4).unsqueeze(3)
+            nc.scalar.copy(wgt_wide1[:], source.to_broadcast([P, 4, 8, GROUP]))
+            spread = sums[1, 1, 1][:].rearrange("p m j -> p (m j)")
+            for a in range(4):
+                nc.tensor.transpose(
+                    spread[:, a * P : (a + 1) * P], wgt_wide1[:, a, :, :].rearrange("p g s -> p (g s)"), identity[:]
+                )
+            nc.scalar.copy(weights[1][:], spread)
 
         def gather(i, c, lo, hi, target):
             offsets = lists[:, (c * J + lo) // GROUP : (c * J + hi) // GROUP]
@@ -162,10 +191,8 @@ def tile_list_prod_bias_kernel(tc, xT, wgt, w, b, offs, out):
                 add_bias(h, u, m, engines[m])
                 store(h, u, slice(m, m + 1))
 
-        for half in range(2):
-            nc.vector.transpose(wgt_turned[:, half, :, :].rearrange("p h r -> p (h r)"), wgt_rows[:, half, :])
-        spread_weights(0, on_v)
-        spread_weights(1, on_s)
+        spread_first()
+        spread_second()
         for i in range(2):
             for c in range(PICKS):
                 gather(i, c, 0, J, early[c][:, i, :])
@@ -191,18 +218,18 @@ def tile_list_prod_bias_kernel(tc, xT, wgt, w, b, offs, out):
         gather_half(3, 1, 1, 8)
         quantise_x(0, 1)
         project(0, 1, 0)
-        round_late(1, 1, 8, on_v)
+        round_late(1, 1, 8, on_s)
         quantise_w(1)
         project(0, 0, 1)
         project(1, 0, 1)
         project(0, 1, 1)
+        finish(0, 0, "vv")
         quantise_x(1, 1)
         project(1, 1, 0)
         project(1, 1, 1)
         keep_first(1, 0, on_s)
         keep_first(0, 1, on_s)
         keep_first(1, 1, on_s)
-        finish(0, 0, "vv")
         finish(1, 0, "ss")
         finish(0, 1, "ss")
         finish(1, 1, "sv")

@@ -44,9 +44,9 @@ def tile_list_prod_bias_kernel(tc, xT, wgt, w, b, offs, out):
         early = [keep.tile([P, 2, J], F32, name="early%d" % c) for c in range(PICKS)]
         late = keep.tile([P, 10, HALF], F32, name="late")
         x_bf = [keep.tile([P, J, PACK], BF16, name="x_bf%d" % c, align_bytes=64) for c in range(PICKS)]
-        x_codes = [keep.tile([P, J], U32, name="x_codes%d" % c, align_bytes=64) for c in range(PICKS)]
+        x_codes = {}
         x_scales = [keep.tile([P, J], U8, name="x_scales%d" % c, align_bytes=64) for c in range(PICKS)]
-        w_second = keep.tile([P, PACK, HALF], F32, name="w_second")
+        w_second = keep.tile([P, PACK, HALF], F32, name="w_second", tag="w_second", align_bytes=64)
         w_raw = [late[:, 3:7, :], w_second[:]]
         w_bf = [keep.tile([P, HALF, PACK], BF16, name="w_bf%d" % u, align_bytes=64) for u in range(2)]
         w_codes = [keep.tile([P, HALF], U32, name="w_codes%d" % u, align_bytes=64) for u in range(2)]
@@ -138,8 +138,11 @@ def tile_list_prod_bias_kernel(tc, xT, wgt, w, b, offs, out):
 
         def quantise_x(c, h):
             cols = slice(h * HALF, (h + 1) * HALF)
+            name = "x_codes%d%d" % (c, h)
+            tag = "w_second" if (c, h) == (0, 1) else name
+            x_codes[c, h] = keep.tile([P, HALF], U32, name=name, tag=tag, align_bytes=64)
             nc.vector.quantize_mx(
-                out=x_codes[c][:, cols].bitcast(FP8X4),
+                out=x_codes[c, h][:].bitcast(FP8X4),
                 scales=x_scales[c][:, cols],
                 in_=x_bf[c][:, cols, :].rearrange("p j i -> p (j i)"),
             )
@@ -157,7 +160,7 @@ def tile_list_prod_bias_kernel(tc, xT, wgt, w, b, offs, out):
                     out=bank(c, h, u, m),
                     lhsT=w_codes[u][:, chan].bitcast(FP8X4),
                     lhsT_scale=w_scales[u][:, chan],
-                    rhs=x_codes[c][:, cols].bitcast(FP8X4),
+                    rhs=x_codes[c, h][:].bitcast(FP8X4),
                     rhs_scale=x_scales[c][:, cols],
                     start=True,
                     stop=True,
@@ -216,20 +219,20 @@ def tile_list_prod_bias_kernel(tc, xT, wgt, w, b, offs, out):
         keep_first(0, 0, on_s)
         gather_half(2, 1, 1, 3)
         gather_half(3, 1, 1, 8)
-        quantise_x(0, 1)
-        project(0, 1, 0)
-        round_late(1, 1, 8, on_s)
         quantise_w(1)
         project(0, 0, 1)
         project(1, 0, 1)
+        quantise_x(0, 1)
+        project(0, 1, 0)
         project(0, 1, 1)
+        round_late(1, 1, 8, on_s)
+        keep_first(0, 1, on_s)
         finish(0, 0, "vv")
         quantise_x(1, 1)
         project(1, 1, 0)
         project(1, 1, 1)
         keep_first(1, 0, on_s)
-        keep_first(0, 1, on_s)
         keep_first(1, 1, on_s)
+        finish(0, 1, "vs")
         finish(1, 0, "ss")
-        finish(0, 1, "ss")
         finish(1, 1, "sv")

@@ -31,11 +31,10 @@ def tile_list_prod_bias_kernel(tc, xT, wgt, w, b, offs, out):
 
         lists = keep.tile([P, PICKS * J // GROUP], U16, name="lists")
         weights = [keep.tile([P, J], F32, name="weights%d" % c, align_bytes=64) for c in range(PICKS)]
-        wgt_rows = keep.tile([P, BLOCK], F32, name="wgt_rows", align_bytes=64)
-        wgt_turned = keep.tile([P, 2, GROUP], F32, name="wgt_turned", align_bytes=64)
-        wgt_wide = keep.tile([P, GROUP, 2, GROUP], F32, name="wgt_wide", align_bytes=64)
-        wgt_rows1 = keep.tile([P, P], F32, name="wgt_rows1")
-        wgt_wide1 = keep.tile([P, 4, 8, GROUP], F32, name="wgt_wide1")
+        wgt_rows = keep.tile([P, P], F32, name="wgt_rows", align_bytes=64)
+        wgt_turned = keep.tile([P, 2, 2, GROUP], F32, name="wgt_turned", align_bytes=64)
+        wgt_wide = keep.tile([P, 8, 2, 2, GROUP], F32, name="wgt_wide", align_bytes=64)
+        wgt_wide1 = keep.tile([P, 8, 8, GROUP], F32, name="wgt_wide1")
         identity = keep.tile([P, P], F32, name="identity")
         ones = keep.tile([P, BLOCK], F32, name="ones")
         ramp = keep.tile([P, BLOCK], F32, name="ramp", align_bytes=64)
@@ -68,9 +67,9 @@ def tile_list_prod_bias_kernel(tc, xT, wgt, w, b, offs, out):
         w_view = w.rearrange("(p i) n -> p i n", i=PACK)
         out_view = out.rearrange("(m p) j -> p m j", p=P)
 
-        head_rows = wgt.rearrange("(g s) j -> g s j", s=GROUP)[:, 0, :]
-        nc.sync.dma_start(wgt_rows[:], head_rows[:, 0:J].rearrange("g (r e) -> g r e", e=BLOCK))
-        nc.sync.dma_start(wgt_rows1[0:32, :], head_rows[:, J : 2 * J].rearrange("g (a e) -> g a e", e=P))
+        nc.sync.dma_start(
+            wgt_rows[:, 0:64], wgt.rearrange("(g s) (r e) -> g s r e", s=GROUP, r=GROUP)[:, 0, :, :]
+        )
         nc.sync.dma_start(rows[0][:], x_view[:, 0, :])
         nc.sync.dma_start(lists[:], offs)
         nc.sync.dma_start(rows[1][:], x_view[:, 1, :])
@@ -82,10 +81,14 @@ def tile_list_prod_bias_kernel(tc, xT, wgt, w, b, offs, out):
             nc.sync.dma_start(bias[:], b.rearrange("(m p) -> p m", p=P))
 
         def spread_first():
-            nc.vector.transpose(wgt_turned[:].rearrange("p h r -> p (h r)"), wgt_rows[:])
-            source = wgt_turned[:].rearrange("p h r -> p r h").unsqueeze(3)
-            nc.vector.tensor_copy(wgt_wide[:], source.to_broadcast([P, GROUP, 2, GROUP]))
-            nc.vector.transpose(weights[0][:], wgt_wide[:].rearrange("p r h s -> p (r h s)"))
+            for half in range(2):
+                nc.vector.transpose(
+                    wgt_turned[:, half, :, :].rearrange("p h r -> p (h r)"),
+                    wgt_rows[:, half * BLOCK : (half + 1) * BLOCK],
+                )
+            source = wgt_turned[:].rearrange("p b h r -> p r b h")[:, 0:8, :, :].unsqueeze(4)
+            nc.vector.tensor_copy(wgt_wide[:], source.to_broadcast([P, 8, 2, 2, GROUP]))
+            nc.vector.transpose(weights[0][:], wgt_wide[:].rearrange("p r b h s -> p (r b h s)"))
 
         def spread_second():
             nc.vector.memset(ones[:], 1.0)
@@ -97,18 +100,22 @@ def tile_list_prod_bias_kernel(tc, xT, wgt, w, b, offs, out):
                 nc.vector.tensor_tensor(
                     identity[part, part], ramp[part, :], ramp_turned[part, :], mybir.AluOpType.is_equal
                 )
-            nc.vector.memset(wgt_rows1[32:64, :], 0.0)
-            nc.vector.memset(wgt_rows1[64:128, :], 0.0)
+            nc.vector.memset(wgt_rows[:, 64:P], 0.0)
             turned = sums[1, 1, 0][:, 0, 0:P]
-            nc.tensor.transpose(turned, wgt_rows1[:], identity[:])
-            source = turned[:, 0:32].rearrange("p (g a) -> p a g", a=4).unsqueeze(3)
-            nc.scalar.copy(wgt_wide1[:], source.to_broadcast([P, 4, 8, GROUP]))
-            spread = sums[1, 1, 1][:].rearrange("p m j -> p (m j)")
-            for a in range(4):
-                nc.tensor.transpose(
-                    spread[:, a * P : (a + 1) * P], wgt_wide1[:, a, :, :].rearrange("p g s -> p (g s)"), identity[:]
-                )
-            nc.scalar.copy(weights[1][:], spread)
+            nc.tensor.transpose(turned, wgt_rows[:], identity[:])
+            source = turned.rearrange("p (g r) -> p r g", r=GROUP)
+            for half in range(2):
+                runs = slice(4 * half, 4 * half + 4)
+                wide = source[:, 8 + 4 * half : 12 + 4 * half, :].unsqueeze(3).to_broadcast([P, 4, 8, GROUP])
+                nc.scalar.copy(wgt_wide1[:, runs, :, :], wide)
+            for half in range(2):
+                spread = sums[0, 1, half][:].rearrange("p m (a j) -> p (m a) j", j=P)
+                for a in range(4):
+                    nc.tensor.transpose(
+                        spread[:, a, :], wgt_wide1[:, 4 * half + a, :, :].rearrange("p g s -> p (g s)"), identity[:]
+                    )
+                target = weights[1][:, half * HALF : (half + 1) * HALF].rearrange("p (a e) -> p a e", e=64)
+                nc.scalar.copy(target, spread[:, :, 0:64])
 
         def gather(i, c, lo, hi, target):
             offsets = lists[:, (c * J + lo) // GROUP : (c * J + hi) // GROUP]
@@ -196,9 +203,11 @@ def tile_list_prod_bias_kernel(tc, xT, wgt, w, b, offs, out):
 
         spread_first()
         spread_second()
-        for i in range(2):
-            for c in range(PICKS):
-                gather(i, c, 0, J, early[c][:, i, :])
+        gather(0, 0, 0, J, early[0][:, 0, :])
+        for h in range(2):
+            gather(0, 1, h * HALF, (h + 1) * HALF, early[1][:, 0, h * HALF : (h + 1) * HALF])
+        for c in range(PICKS):
+            gather(1, c, 0, J, early[c][:, 1, :])
         for c in range(PICKS):
             round_early(c, on_s)
         gather(2, 0, 0, J, late[:, 0:2, :].rearrange("p s j -> p (s j)"))

@@ -68,7 +68,7 @@ def tile_list_prod_bias_kernel(tc, xT, wgt, w, b, offs, out):
         out_view = out.rearrange("(m p) j -> p m j", p=P)
 
         nc.sync.dma_start(
-            wgt_rows[:, 0:64], wgt.rearrange("(g s) (r e) -> g s r e", s=GROUP, r=GROUP)[:, 0, :, :]
+            wgt_rows[:, 0:64], wgt.rearrange("p (h e) -> (p h) e", h=PICKS)[0 : PICKS * P : GROUP + 1, :]
         )
         nc.sync.dma_start(rows[0][:], x_view[:, 0, :])
         nc.sync.dma_start(lists[:], offs)

@@ -30,7 +30,7 @@ def tile_list_prod_bias_kernel(tc, xT, wgt, w, b, offs, out):
         psum = ctx.enter_context(tc.psum_pool(name="psum", bufs=1))
 
         lists = keep.tile([P, PICKS * J // GROUP], U16, name="lists")
-        weights = [keep.tile([P, J], F32, name="weights%d" % c, align_bytes=64) for c in range(PICKS)]
+        weights = keep.tile([P, PICKS * J], F32, name="weights", align_bytes=64)
         wgt_rows = keep.tile([P, P], F32, name="wgt_rows", align_bytes=64)
         wgt_turned = keep.tile([P, 2, 2, GROUP], F32, name="wgt_turned", align_bytes=64)
         wgt_wide = keep.tile([P, 8, 2, 2, GROUP], F32, name="wgt_wide", align_bytes=64)
@@ -41,12 +41,14 @@ def tile_list_prod_bias_kernel(tc, xT, wgt, w, b, offs, out):
         ramp_turned = keep.tile([P, BLOCK], F32, name="ramp_turned", align_bytes=64)
         rows = [keep.tile([P, T], F32, name="rows%d" % i) for i in range(PACK)]
         early = [keep.tile([P, 2, J], F32, name="early%d" % c) for c in range(PICKS)]
-        late = keep.tile([P, 10, HALF], F32, name="late")
+        late = keep.tile([P, 11, HALF], F32, name="late")
         x_bf = [keep.tile([P, J, PACK], BF16, name="x_bf%d" % c, align_bytes=64) for c in range(PICKS)]
         x_codes = {}
         x_scales = [keep.tile([P, J], U8, name="x_scales%d" % c, align_bytes=64) for c in range(PICKS)]
         w_second = keep.tile([P, PACK, HALF], F32, name="w_second", tag="w_second", align_bytes=64)
-        w_raw = [late[:, 3:7, :], w_second[:]]
+        w_start = 3 * HALF + P
+        w_first = late[:].rearrange("p s j -> p (s j)")[:, w_start : w_start + PACK * HALF]
+        w_raw = [w_first.rearrange("p (i n) -> p i n", i=PACK), w_second[:]]
         w_bf = [keep.tile([P, HALF, PACK], BF16, name="w_bf%d" % u, align_bytes=64) for u in range(2)]
         w_codes = [keep.tile([P, HALF], U32, name="w_codes%d" % u, align_bytes=64) for u in range(2)]
         w_scales = [keep.tile([P, HALF], U8, name="w_scales%d" % u, align_bytes=64) for u in range(2)]
@@ -59,7 +61,8 @@ def tile_list_prod_bias_kernel(tc, xT, wgt, w, b, offs, out):
             for u in range(2):
                 for c in range(PICKS):
                     sums[c, h, u] = psum.tile([P, 2, HALF], F32, name="sums%d%d%d" % (c, h, u))
-                first[h, u] = keep.tile([P, 2, HALF], F32, name="first%d%d" % (h, u))
+                if (h, u) != (1, 0):
+                    first[h, u] = keep.tile([P, 2, HALF], F32, name="first%d%d" % (h, u), tag="first%d%d" % (h, u))
                 product[h, u] = keep.tile([P, 2, HALF], F32, name="product%d%d" % (h, u))
                 result[h, u] = keep.tile([P, 2, HALF], F32, name="result%d%d" % (h, u))
 
@@ -88,7 +91,7 @@ def tile_list_prod_bias_kernel(tc, xT, wgt, w, b, offs, out):
                 )
             source = wgt_turned[:].rearrange("p b h r -> p r b h")[:, 0:8, :, :].unsqueeze(4)
             nc.vector.tensor_copy(wgt_wide[:], source.to_broadcast([P, 8, 2, 2, GROUP]))
-            nc.vector.transpose(weights[0][:], wgt_wide[:].rearrange("p r b h s -> p (r b h s)"))
+            nc.vector.transpose(weights[:, 0:J], wgt_wide[:].rearrange("p r b h s -> p (r b h s)"))
 
         def spread_second():
             nc.vector.memset(ones[:], 1.0)
@@ -114,12 +117,12 @@ def tile_list_prod_bias_kernel(tc, xT, wgt, w, b, offs, out):
                     nc.tensor.transpose(
                         spread[:, a, :], wgt_wide1[:, 4 * half + a, :, :].rearrange("p g s -> p (g s)"), identity[:]
                     )
-                target = weights[1][:, half * HALF : (half + 1) * HALF].rearrange("p (a e) -> p a e", e=64)
+                target = weights[:, J + half * HALF : J + (half + 1) * HALF].rearrange("p (a e) -> p a e", e=64)
                 nc.scalar.copy(target, spread[:, :, 0:64])
 
         def gather(i, c, lo, hi, target):
             offsets = lists[:, (c * J + lo) // GROUP : (c * J + hi) // GROUP]
-            nc.vector.tensor_tensor(target, rows[i][:].indirect(offsets), weights[c][:, lo:hi], MULT)
+            nc.vector.tensor_tensor(target, rows[i][:].indirect(offsets), weights[:, c * J + lo : c * J + hi], MULT)
 
         def gather_half(i, c, h, slot):
             gather(i, c, h * HALF, (h + 1) * HALF, late[:, slot, :])
@@ -127,26 +130,28 @@ def tile_list_prod_bias_kernel(tc, xT, wgt, w, b, offs, out):
         def round_early(c, copy):
             copy(x_bf[c][:, :, 0:2], early[c][:].rearrange("p i j -> p j i"))
 
-        def round_late(c, h, slot, copy):
+        def round_late(c, h, slot, copy, lo=0, hi=HALF):
             a = PICKS * c + h
-            pair = late[:, a : slot + 1 : slot - a, :]
-            copy(x_bf[c][:, h * HALF : (h + 1) * HALF, 2:4], pair.rearrange("p i j -> p j i"))
+            pair = late[:, a : slot + 1 : slot - a, lo:hi]
+            copy(x_bf[c][:, h * HALF + lo : h * HALF + hi, 2:4], pair.rearrange("p i j -> p j i"))
 
-        def round_w(u, copy):
+        def round_w(u, copy, lo=0, hi=HALF):
             copy(
-                w_bf[u][:].rearrange("p (a e) i -> p a i e", e=4),
-                w_raw[u].rearrange("p i (a e) -> p a i e", e=4),
+                w_bf[u][:, lo:hi, :].rearrange("p (a e) i -> p a i e", e=4),
+                w_raw[u][:, :, lo:hi].rearrange("p i (a e) -> p a i e", e=4),
             )
 
-        def quantise_w(u):
+        def quantise_w(u, lo=0, hi=HALF):
             nc.vector.quantize_mx(
-                out=w_codes[u][:].bitcast(FP8X4), scales=w_scales[u][:], in_=w_bf[u][:].rearrange("p n i -> p (n i)")
+                out=w_codes[u][:, lo:hi].bitcast(FP8X4),
+                scales=w_scales[u][:, lo:hi],
+                in_=w_bf[u][:, lo:hi, :].rearrange("p n i -> p (n i)"),
             )
 
         def quantise_x(c, h):
             cols = slice(h * HALF, (h + 1) * HALF)
             name = "x_codes%d%d" % (c, h)
-            tag = "w_second" if (c, h) == (0, 1) else name
+            tag = name
             x_codes[c, h] = keep.tile([P, HALF], U32, name=name, tag=tag, align_bytes=64)
             nc.vector.quantize_mx(
                 out=x_codes[c, h][:].bitcast(FP8X4),
@@ -155,13 +160,17 @@ def tile_list_prod_bias_kernel(tc, xT, wgt, w, b, offs, out):
             )
 
         def bank(c, h, u, m):
-            if (c, h, u, m) == (1, 1, 1, 1):
+            if (c, h, u, m) == (0, 0, 0, 0):
+                return sums[1, 1, 1][:, 1, :]
+            if (c, h, u, m) == (0, 0, 1, 1):
                 return sums[0, 0, 0][:, 0, :]
+            if (c, h, u, m) == (1, 1, 1, 1):
+                return sums[1, 0, 0][:, 0, :]
             return sums[c, h, u][:, m, :]
 
-        def project(c, h, u):
+        def project(c, h, u, ms=(0, 1)):
             cols = slice(h * HALF, (h + 1) * HALF)
-            for m in range(2):
+            for m in ms:
                 chan = slice(m * P, (m + 1) * P)
                 nc.tensor.matmul_mx(
                     out=bank(c, h, u, m),
@@ -174,7 +183,12 @@ def tile_list_prod_bias_kernel(tc, xT, wgt, w, b, offs, out):
                 )
 
         def keep_first(h, u, copy):
+            if (h, u) == (1, 0):
+                first[h, u] = keep.tile([P, 2, HALF], F32, name="first10", tag="first00")
             copy(first[h, u][:], sums[0, h, u][:])
+
+        def keep_piece(h, u, m):
+            nc.scalar.copy(first[h, u][:, m, :], bank(0, h, u, m))
 
         def multiply(h, u, m):
             nc.vector.tensor_tensor(product[h, u][:, m, :], bank(1, h, u, m), first[h, u][:, m, :], MULT)
@@ -195,6 +209,10 @@ def tile_list_prod_bias_kernel(tc, xT, wgt, w, b, offs, out):
 
         on_v = nc.vector.tensor_copy
         on_s = nc.scalar.copy
+        def biased(h, u, m, engine):
+            add_bias(h, u, m, engine)
+            store(h, u, slice(m, m + 1))
+
         def finish(h, u, engines):
             for m in range(2):
                 multiply(h, u, m)
@@ -210,38 +228,55 @@ def tile_list_prod_bias_kernel(tc, xT, wgt, w, b, offs, out):
             gather(1, c, 0, J, early[c][:, 1, :])
         for c in range(PICKS):
             round_early(c, on_s)
-        gather(2, 0, 0, J, late[:, 0:2, :].rearrange("p s j -> p (s j)"))
-        gather_half(2, 1, 0, 2)
-        gather_half(3, 0, 0, 7)
-        round_late(0, 0, 7, on_s)
-        gather_half(3, 1, 0, 8)
-        round_late(1, 0, 8, on_s)
-        gather_half(3, 0, 1, 9)
-        round_late(0, 1, 9, on_s)
-        round_w(0, on_v)
+        gather(2, 0, 0, J + HALF + P, late[:].rearrange("p s j -> p (s j)")[:, 0 : J + HALF + P])
+        for lo in range(0, HALF, P):
+            gather(3, 0, lo, lo + P, late[:, 8, lo : lo + P])
+            round_late(0, 0, 8, on_s, lo, lo + P)
+        gather_half(3, 1, 0, 9)
+        round_late(1, 0, 9, on_s)
+        gather_half(3, 0, 1, 10)
+        round_late(0, 1, 10, on_s)
+        round_w(0, on_v, 0, P)
+        round_w(0, on_v, P, HALF)
         quantise_x(0, 0)
-        quantise_w(0)
+        quantise_w(0, 0, P)
         quantise_x(1, 0)
-        project(0, 0, 0)
-        project(1, 0, 0)
+        quantise_w(0, P, HALF)
+        quantise_x(0, 1)
+        for m in range(2):
+            project(0, 0, 0, (m,))
+            project(1, 0, 0, (m,))
+        project(0, 1, 0)
         round_w(1, on_s)
-        keep_first(0, 0, on_s)
-        gather_half(2, 1, 1, 3)
-        gather_half(3, 1, 1, 8)
+        keep_piece(0, 0, 0)
+        keep_piece(0, 0, 1)
+        gather(2, 1, HALF + P, J, late[:, 3, P:HALF])
+        gather_half(3, 1, 1, 9)
         quantise_w(1)
         project(0, 0, 1)
         project(1, 0, 1)
-        quantise_x(0, 1)
-        project(0, 1, 0)
         project(0, 1, 1)
-        round_late(1, 1, 8, on_s)
-        keep_first(0, 1, on_s)
-        finish(0, 0, "vv")
+        round_late(1, 1, 9, on_s)
+        keep_piece(0, 1, 0)
+        keep_piece(0, 1, 1)
+        multiply(0, 0, 0)
+        multiply(0, 0, 1)
+        biased(0, 0, 0, "v")
         quantise_x(1, 1)
+        biased(0, 0, 1, "v")
         project(1, 1, 0)
         project(1, 1, 1)
         keep_first(1, 0, on_s)
         keep_first(1, 1, on_s)
-        finish(0, 1, "vs")
-        finish(1, 0, "ss")
-        finish(1, 1, "sv")
+        multiply(0, 1, 0)
+        multiply(0, 1, 1)
+        biased(0, 1, 0, "v")
+        biased(0, 1, 1, "s")
+        multiply(1, 0, 0)
+        multiply(1, 0, 1)
+        biased(1, 0, 0, "s")
+        biased(1, 0, 1, "s")
+        multiply(1, 1, 0)
+        multiply(1, 1, 1)
+        biased(1, 1, 0, "s")
+        biased(1, 1, 1, "v")

from contextlib import ExitStack

import concourse.mybir as mybir

K, N, T, J = 512, 512, 2048, 512
FLOPS = 2 * 2 * K * N * J

F32 = mybir.dt.float32
BF16 = mybir.dt.bfloat16
U32 = mybir.dt.uint32
U16 = mybir.dt.uint16
U8 = mybir.dt.uint8
FP8X4 = mybir.dt.float8_e4m3fn_x4
MULT = mybir.AluOpType.mult
ADD = mybir.AluOpType.add
IDENTITY = mybir.ActivationFunctionType.Identity

P = 128
PACK = 4
PICKS = 2
HALF = J // 2
GROUP = 16
BLOCK = 32


def tile_list_prod_bias_kernel(tc, xT, wgt, w, b, offs, out):
    nc = tc.nc
    with ExitStack() as ctx:
        keep = ctx.enter_context(tc.tile_pool(name="keep", bufs=1))
        psum = ctx.enter_context(tc.psum_pool(name="psum", bufs=1))

        lists = keep.tile([P, PICKS * J // GROUP], U16, name="lists")
        weights = keep.tile([P, PICKS * J], F32, name="weights", align_bytes=64)
        wgt_rows = keep.tile([P, P], F32, name="wgt_rows", align_bytes=64)
        wgt_turned = keep.tile([P, 2, 2, GROUP], F32, name="wgt_turned", align_bytes=64)
        wgt_wide = keep.tile([P, 8, 2, 2, GROUP], F32, name="wgt_wide", align_bytes=64)
        wgt_wide1 = keep.tile([P, 8, 8, GROUP], F32, name="wgt_wide1")
        identity = keep.tile([P, P], F32, name="identity")
        ones = keep.tile([P, BLOCK], F32, name="ones")
        ramp = keep.tile([P, BLOCK], F32, name="ramp", align_bytes=64)
        ramp_turned = keep.tile([P, BLOCK], F32, name="ramp_turned", align_bytes=64)
        rows = [keep.tile([P, T], F32, name="rows%d" % i) for i in range(PACK)]
        early = [keep.tile([P, 2, J], F32, name="early%d" % c) for c in range(PICKS)]
        late = keep.tile([P, 11, HALF], F32, name="late")
        x_bf = [keep.tile([P, J, PACK], BF16, name="x_bf%d" % c, align_bytes=64) for c in range(PICKS)]
        x_codes = {}
        x_scales = [keep.tile([P, J], U8, name="x_scales%d" % c, align_bytes=64) for c in range(PICKS)]
        w_second = keep.tile([P, PACK, HALF], F32, name="w_second", tag="w_second", align_bytes=64)
        w_start = 3 * HALF + P
        w_first = late[:].rearrange("p s j -> p (s j)")[:, w_start : w_start + PACK * HALF]
        w_raw = [w_first.rearrange("p (i n) -> p i n", i=PACK), w_second[:]]
        w_bf = [keep.tile([P, HALF, PACK], BF16, name="w_bf%d" % u, align_bytes=64) for u in range(2)]
        w_codes = [keep.tile([P, HALF], U32, name="w_codes%d" % u, align_bytes=64) for u in range(2)]
        w_scales = [keep.tile([P, HALF], U8, name="w_scales%d" % u, align_bytes=64) for u in range(2)]
        bias = keep.tile([P, N // P], F32, name="bias")
        sums = {}
        first = {}
        product = {}
        result = {}
        for h in range(2):
            for u in range(2):
                for c in range(PICKS):
                    sums[c, h, u] = psum.tile([P, 2, HALF], F32, name="sums%d%d%d" % (c, h, u))
                if (h, u) != (1, 0):
                    first[h, u] = keep.tile([P, 2, HALF], F32, name="first%d%d" % (h, u), tag="first%d%d" % (h, u))
                product[h, u] = keep.tile([P, 2, HALF], F32, name="product%d%d" % (h, u))
                result[h, u] = keep.tile([P, 2, HALF], F32, name="result%d%d" % (h, u))

        x_view = xT.rearrange("(p i) t -> p i t", i=PACK)
        w_view = w.rearrange("(p i) n -> p i n", i=PACK)
        out_view = out.rearrange("(m p) j -> p m j", p=P)

        nc.sync.dma_start(
            wgt_rows[:, 0:64], wgt.rearrange("p (h e) -> (p h) e", h=PICKS)[0 : PICKS * P : GROUP + 1, :]
        )
        nc.sync.dma_start(rows[0][:], x_view[:, 0, :])
        nc.sync.dma_start(lists[:], offs)
        nc.sync.dma_start(rows[1][:], x_view[:, 1, :])
        nc.sync.dma_start(rows[2][:], x_view[:, 2, :])
        nc.sync.dma_start(rows[3][:], x_view[:, 3, :])
        nc.sync.dma_start(w_raw[0], w_view[:, :, 0:HALF])
        nc.sync.dma_start(w_raw[1], w_view[:, :, HALF:N])
        with nc.allow_non_contiguous_dma(reason="one bias value to a partition"):
            nc.sync.dma_start(bias[:], b.rearrange("(m p) -> p m", p=P))

        def spread_first():
            for half in range(2):
                nc.vector.transpose(
                    wgt_turned[:, half, :, :].rearrange("p h r -> p (h r)"),
                    wgt_rows[:, half * BLOCK : (half + 1) * BLOCK],
                )
            source = wgt_turned[:].rearrange("p b h r -> p r b h")[:, 0:8, :, :].unsqueeze(4)
            nc.vector.tensor_copy(wgt_wide[:], source.to_broadcast([P, 8, 2, 2, GROUP]))
            nc.vector.transpose(weights[:, 0:J], wgt_wide[:].rearrange("p r b h s -> p (r b h s)"))

        def spread_second():
            nc.vector.memset(ones[:], 1.0)
            nc.vector.memset(identity[:], 0.0)
            nc.vector.tensor_tensor_scan(ramp[:], ones[:], ones[:], 0.0, MULT, ADD)
            nc.vector.transpose(ramp_turned[:], ramp[:])
            for q in range(P // BLOCK):
                part = slice(q * BLOCK, (q + 1) * BLOCK)
                nc.vector.tensor_tensor(
                    identity[part, part], ramp[part, :], ramp_turned[part, :], mybir.AluOpType.is_equal
                )
            nc.vector.memset(wgt_rows[:, 64:P], 0.0)
            turned = sums[1, 1, 0][:, 0, 0:P]
            nc.tensor.transpose(turned, wgt_rows[:], identity[:])
            source = turned.rearrange("p (g r) -> p r g", r=GROUP)
            for half in range(2):
                runs = slice(4 * half, 4 * half + 4)
                wide = source[:, 8 + 4 * half : 12 + 4 * half, :].unsqueeze(3).to_broadcast([P, 4, 8, GROUP])
                nc.scalar.copy(wgt_wide1[:, runs, :, :], wide)
            for half in range(2):
                spread = sums[0, 1, half][:].rearrange("p m (a j) -> p (m a) j", j=P)
                for a in range(4):
                    nc.tensor.transpose(
                        spread[:, a, :], wgt_wide1[:, 4 * half + a, :, :].rearrange("p g s -> p (g s)"), identity[:]
                    )
                target = weights[:, J + half * HALF : J + (half + 1) * HALF].rearrange("p (a e) -> p a e", e=64)
                nc.scalar.copy(target, spread[:, :, 0:64])

        def gather(i, c, lo, hi, target):
            offsets = lists[:, (c * J + lo) // GROUP : (c * J + hi) // GROUP]
            nc.vector.tensor_tensor(target, rows[i][:].indirect(offsets), weights[:, c * J + lo : c * J + hi], MULT)

        def gather_half(i, c, h, slot):
            gather(i, c, h * HALF, (h + 1) * HALF, late[:, slot, :])

        def round_early(c, copy):
            copy(x_bf[c][:, :, 0:2], early[c][:].rearrange("p i j -> p j i"))

        def round_late(c, h, slot, copy, lo=0, hi=HALF):
            a = PICKS * c + h
            pair = late[:, a : slot + 1 : slot - a, lo:hi]
            copy(x_bf[c][:, h * HALF + lo : h * HALF + hi, 2:4], pair.rearrange("p i j -> p j i"))

        def round_w(u, copy, lo=0, hi=HALF):
            copy(
                w_bf[u][:, lo:hi, :].rearrange("p (a e) i -> p a i e", e=4),
                w_raw[u][:, :, lo:hi].rearrange("p i (a e) -> p a i e", e=4),
            )

        def quantise_w(u, lo=0, hi=HALF):
            nc.vector.quantize_mx(
                out=w_codes[u][:, lo:hi].bitcast(FP8X4),
                scales=w_scales[u][:, lo:hi],
                in_=w_bf[u][:, lo:hi, :].rearrange("p n i -> p (n i)"),
            )

        def quantise_x(c, h):
            cols = slice(h * HALF, (h + 1) * HALF)
            name = "x_codes%d%d" % (c, h)
            tag = name
            x_codes[c, h] = keep.tile([P, HALF], U32, name=name, tag=tag, align_bytes=64)
            nc.vector.quantize_mx(
                out=x_codes[c, h][:].bitcast(FP8X4),
                scales=x_scales[c][:, cols],
                in_=x_bf[c][:, cols, :].rearrange("p j i -> p (j i)"),
            )

        def bank(c, h, u, m):
            if (c, h, u, m) == (0, 0, 0, 0):
                return sums[1, 1, 1][:, 1, :]
            if (c, h, u, m) == (0, 0, 1, 1):
                return sums[0, 0, 0][:, 0, :]
            if (c, h, u, m) == (1, 1, 1, 1):
                return sums[1, 0, 0][:, 0, :]
            return sums[c, h, u][:, m, :]

        def project(c, h, u, ms=(0, 1)):
            cols = slice(h * HALF, (h + 1) * HALF)
            for m in ms:
                chan = slice(m * P, (m + 1) * P)
                nc.tensor.matmul_mx(
                    out=bank(c, h, u, m),
                    lhsT=w_codes[u][:, chan].bitcast(FP8X4),
                    lhsT_scale=w_scales[u][:, chan],
                    rhs=x_codes[c, h][:].bitcast(FP8X4),
                    rhs_scale=x_scales[c][:, cols],
                    start=True,
                    stop=True,
                )

        def keep_first(h, u, copy):
            if (h, u) == (1, 0):
                first[h, u] = keep.tile([P, 2, HALF], F32, name="first10", tag="first00")
            copy(first[h, u][:], sums[0, h, u][:])

        def keep_piece(h, u, m):
            nc.scalar.copy(first[h, u][:, m, :], bank(0, h, u, m))

        def multiply(h, u, m):
            nc.vector.tensor_tensor(product[h, u][:, m, :], bank(1, h, u, m), first[h, u][:, m, :], MULT)

        def add_bias(h, u, m, engine):
            column = bias[:, 2 * u + m : 2 * u + m + 1]
            if engine == "v":
                nc.vector.tensor_scalar(result[h, u][:, m, :], product[h, u][:, m, :], column, None, ADD)
            elif engine == "g":
                nc.gpsimd.tensor_scalar(result[h, u][:, m, :], product[h, u][:, m, :], 1.0, column, MULT, ADD)
            else:
                nc.scalar.activation(result[h, u][:, m, :], product[h, u][:, m, :], IDENTITY, bias=column)

        def store(h, u, ms):
            nc.sync.dma_start(
                out_view[:, 2 * u + ms.start : 2 * u + ms.stop, h * HALF : (h + 1) * HALF], result[h, u][:, ms, :]
            )

        on_v = nc.vector.tensor_copy
        on_s = nc.scalar.copy
        def biased(h, u, m, engine):
            add_bias(h, u, m, engine)
            store(h, u, slice(m, m + 1))

        def finish(h, u, engines):
            for m in range(2):
                multiply(h, u, m)
                add_bias(h, u, m, engines[m])
                store(h, u, slice(m, m + 1))

        spread_first()
        spread_second()
        gather(0, 0, 0, J, early[0][:, 0, :])
        for h in range(2):
            gather(0, 1, h * HALF, (h + 1) * HALF, early[1][:, 0, h * HALF : (h + 1) * HALF])
        for c in range(PICKS):
            gather(1, c, 0, J, early[c][:, 1, :])
        for c in range(PICKS):
            round_early(c, on_s)
        gather(2, 0, 0, J + HALF + P, late[:].rearrange("p s j -> p (s j)")[:, 0 : J + HALF + P])
        for lo in range(0, HALF, P):
            gather(3, 0, lo, lo + P, late[:, 8, lo : lo + P])
            round_late(0, 0, 8, on_s, lo, lo + P)
        gather_half(3, 1, 0, 9)
        round_late(1, 0, 9, on_s)
        gather_half(3, 0, 1, 10)
        round_late(0, 1, 10, on_s)
        round_w(0, on_v, 0, P)
        round_w(0, on_v, P, HALF)
        quantise_x(0, 0)
        quantise_w(0, 0, P)
        quantise_x(1, 0)
        quantise_w(0, P, HALF)
        quantise_x(0, 1)
        for m in range(2):
            project(0, 0, 0, (m,))
            project(1, 0, 0, (m,))
        project(0, 1, 0)
        round_w(1, on_s)
        keep_piece(0, 0, 0)
        keep_piece(0, 0, 1)
        gather(2, 1, HALF + P, J, late[:, 3, P:HALF])
        gather_half(3, 1, 1, 9)
        quantise_w(1)
        project(0, 0, 1)
        project(1, 0, 1)
        project(0, 1, 1)
        round_late(1, 1, 9, on_s)
        keep_piece(0, 1, 0)
        keep_piece(0, 1, 1)
        multiply(0, 0, 0)
        multiply(0, 0, 1)
        biased(0, 0, 0, "v")
        quantise_x(1, 1)
        biased(0, 0, 1, "v")
        project(1, 1, 0)
        project(1, 1, 1)
        keep_first(1, 0, on_s)
        keep_first(1, 1, on_s)
        multiply(0, 1, 0)
        multiply(0, 1, 1)
        biased(0, 1, 0, "v")
        biased(0, 1, 1, "s")
        multiply(1, 0, 0)
        multiply(1, 0, 1)
        biased(1, 0, 0, "s")
        biased(1, 0, 1, "s")
        multiply(1, 1, 0)
        multiply(1, 1, 1)
        biased(1, 1, 0, "s")
        biased(1, 1, 1, "v")
